import numpy as np
import ml_dtypes


def mxq(x, axis, fmt="e4m3"):
    dtype, down = {"e4m3": (ml_dtypes.float8_e4m3fn, 7), "e5m2": (ml_dtypes.float8_e5m2, 14)}[fmt]
    v = np.moveaxis(np.asarray(x, np.float32).astype(ml_dtypes.bfloat16).astype(np.float64), axis, -1)
    blocks = v.reshape(v.shape[:-1] + (-1, 32))
    amax = np.abs(blocks).max(-1, keepdims=True)
    byte = np.maximum(np.where(amax > 0, np.frexp(amax)[1] - 1 + 127, 0) - down, 1)
    scale = np.exp2(byte - 127.0)
    codes = (blocks / scale).astype(np.float32).astype(dtype).astype(np.float64)
    return np.moveaxis((codes * scale).reshape(v.shape), -1, axis)


WIDE = False


def mx_kscale(k):
    if not WIDE:
        return np.ones(k)
    levels = np.array([10, -10, 5, -5, 0])
    if k % 512:
        return np.exp2(np.random.permutation(np.resize(levels, k // 32))).repeat(32)
    a = np.empty((k // 512, 16))
    for p in range(k // 512):
        a[p, :8] = np.random.permutation(np.resize(levels, 8))
        for g in range(8):
            far = levels[np.abs(levels - a[p, g]) >= 10]
            a[p, g + 8] = far[np.random.randint(len(far))]
    return np.exp2(a.ravel()).repeat(32)


def f64(x):
    return np.asarray(x).astype(np.float64)


def striped8(idx):
    return np.asarray(idx).reshape(8, -1, 16).transpose(0, 2, 1).reshape(128, -1).astype(np.uint16)


def unstriped8(offs):
    return offs.reshape(8, 16, -1).transpose(0, 2, 1).reshape(8, -1).astype(np.int64)


def pick8(x, idx, run):
    r = np.arange(len(x))
    return x[r[:, None], idx[r % (8 * run) // run]]


E2M1 = np.array([0.0, 0.5, 1.0, 1.5, 2.0, 3.0, 4.0, 6.0, -0.0, -0.5, -1.0, -1.5, -2.0, -3.0, -4.0, -6.0])


def pack_weight(w, fmt):
    k, n = w.shape
    w = f64(np.asarray(w, np.float32).astype(ml_dtypes.bfloat16)).reshape(k // 32, 32, n)
    amax = np.abs(w).max(1)
    if fmt == "e4m3":
        byte = np.frexp(amax)[1] - 1 + 127 - 7
    else:
        mant, ex = np.frexp(amax / 6.0)
        byte = np.where(mant > 0.5, ex, ex - 1) + 127
    byte = np.clip(np.where(amax > 0, byte, 1), 1, 254)
    scaled = (w * np.exp2(127.0 - byte)[:, None, :]).reshape(k, n).astype(np.float32)
    by_word = np.ascontiguousarray(scaled.reshape(k // 512, 128, 4, n).transpose(0, 1, 3, 2))
    if fmt == "e4m3":
        words = by_word.astype(ml_dtypes.float8_e4m3fn).view(np.uint8)
    else:
        c = by_word.astype(ml_dtypes.float4_e2m1fn).view(np.uint8) & 0xF
        words = (c[..., 0::2] | (c[..., 1::2] << 4)).reshape(k // 512, 128, 2 * n)
    return np.ascontiguousarray(words), np.ascontiguousarray(byte.astype(np.uint8).reshape(k // 512, 16, n))


def unpack_weight(words, scales, fmt):
    g, _, n = scales.shape
    words = np.ascontiguousarray(words).reshape(g, 128, n, -1)
    if fmt == "e4m3":
        vals = words.view(ml_dtypes.float8_e4m3fn).astype(np.float64)
    else:
        nib = np.empty((g, 128, n, 4), np.uint8)
        nib[..., 0::2] = words & 0xF
        nib[..., 1::2] = words >> 4
        vals = E2M1[nib]
    vals = vals * np.repeat(np.exp2(scales.astype(np.float64) - 127.0), 8, axis=1)[..., None]
    return vals.transpose(0, 1, 3, 2).reshape(g * 512, n)


def softplus(v):
    return np.log(1.0 + np.exp(v))


D, T, I, Q = 512, 1024, 512, 128


def setup_inputs():
    n = np.random.standard_normal
    idx = np.stack([np.random.permutation(T)[:I] for _ in range(8)])
    idx2 = np.stack([np.random.permutation(T)[:I] for _ in range(8)])
    idx3 = np.stack([np.random.permutation(T)[:I] for _ in range(8)])
    fd = mx_kscale(D)
    keysp = pack_weight(n((D, T)) / fd[:, None], "e4m3")
    return {
        "query": (n((D, Q)) * 0.9 / np.sqrt(D) * fd[:, None]).astype(np.float32),
        "query2": (n((D, Q)) * 0.9 / np.sqrt(D) * fd[:, None]).astype(np.float32),
        "keys_words": keysp[0],
        "keys_scales": keysp[1],
        "lam": (np.random.uniform(1.0, 2.0, (Q, 1))).astype(np.float32),
        "old": (np.random.uniform(0.3, 1.7, (Q, T))).astype(np.float32),
        "base": (0.5 * n((Q, T))).astype(np.float32),
        "offs": striped8(idx),
        "offs2": striped8(idx2),
        "offs3": striped8(idx3),
    }


def reference(query, query2, keys_words, keys_scales, lam, old, base, offs, offs2, offs3):
    idx = unstriped8(offs)
    idx2 = unstriped8(offs2)
    idx3 = unstriped8(offs3)
    keysu = unpack_weight(keys_words, keys_scales, "e4m3")
    queryq = mxq(f64(query), 0, "e4m3")
    a = queryq.T @ keysu
    query2q = mxq(f64(query2), 0, "e4m3")
    b = query2q.T @ keysu
    ra = np.sqrt(softplus(pick8(a, idx, 16)) * softplus(pick8(b, idx, 16)) + 0.1)
    w = ra * f64(lam) - np.abs(pick8(a, idx, 16) - pick8(b, idx, 16))
    ws = w * pick8(f64(old), idx2, 16)
    f1 = np.zeros((Q, T))
    f1[np.arange(Q)[:, None], idx3[np.arange(Q) % 128 // 16]] = ws
    y = f64(base) + f1
    return y

from contextlib import ExitStack

import concourse.mybir as mybir

F32 = mybir.dt.float32
BF16 = mybir.dt.bfloat16
I32 = mybir.dt.int32
U32 = mybir.dt.uint32
U16 = mybir.dt.uint16
U8 = mybir.dt.uint8
FP8X4 = mybir.dt.float8_e4m3fn_x4
ALU = mybir.AluOpType
ACT = mybir.ActivationFunctionType

P = 128
PACK = 4
D, T, SLOTS, Q = 512, 1024, 512, 128
LIST_COLS = SLOTS // 16
N_MM = 256
KEY_LOADS = 2
STORES = 4
SOFTPLUS_CAP = 40.0
FLOPS = 2 * 2 * D * Q * T


def tile_attend_agreeingtwo_lean_timesold_heads_kernel(
    tc, query, query2, keys_words, keys_scales, lam, old, base, offs, offs2, offs3, out
):
    nc = tc.nc
    with ExitStack() as ctx:
        pool = ctx.enter_context(tc.tile_pool(name="sb", bufs=1))
        psum = ctx.enter_context(tc.psum_pool(name="ps", bufs=1))

        key_cols = T // KEY_LOADS
        list_ab = pool.tile([P, LIST_COLS], U16, name="list_ab")
        list_old = pool.tile([P, LIST_COLS], U16, name="list_old")
        list_out = pool.tile([P, LIST_COLS], U16, name="list_out")
        q_raw = [pool.tile([P, PACK, Q], F32, name="q_raw%d" % j) for j in range(2)]
        k_words = [pool.tile([P, key_cols], U32, name="k_words%d" % j, tag="keys%d" % j, align_bytes=64) for j in range(KEY_LOADS)]
        k_scales = pool.tile([P, T], U8, name="k_scales", align_bytes=64)
        lam_sb = pool.tile([P, 1], F32, name="lam_sb")
        old_sb = pool.tile([P, T], F32, name="old_sb")
        base_sb = pool.tile([P, T], F32, name="base_sb")
        placed = pool.tile([P, T], F32, name="placed")

        nc.vector.memset(k_scales[:].bitcast(U32), 0)
        words = keys_words[0].rearrange("p n t -> p (n t)")
        nc.sync.dma_start(list_ab[:], offs)
        nc.sync.dma_start(q_raw[0][:], query.rearrange("(p j) w -> p j w", j=PACK))
        for quad in range(4):
            nc.scalar.dma_start(
                k_scales[32 * quad : 32 * quad + 4, :].bitcast(I32),
                keys_scales[0, 4 * quad : 4 * quad + 4, :].bitcast(I32),
            )
        nc.sync.dma_start(k_words[0][:].bitcast(I32), words[:, : PACK * key_cols].bitcast(I32))
        nc.sync.dma_start(q_raw[1][:], query2.rearrange("(p j) w -> p j w", j=PACK))
        nc.sync.dma_start(k_words[1][:].bitcast(I32), words[:, PACK * key_cols :].bitcast(I32))
        nc.sync.dma_start(old_sb[:], old)
        nc.sync.dma_start(list_old[:], offs2)
        nc.sync.dma_start(lam_sb[:], lam)
        nc.sync.dma_start(list_out[:], offs3)
        nc.sync.dma_start(base_sb[:], base)
        nc.vector.memset(placed[:], 0.0)

        q_words, q_scales = [], []
        for j in range(2):
            grouped = pool.tile([P, Q, PACK], BF16, name="grouped%d" % j, align_bytes=64)
            nc.vector.tensor_copy(grouped[:], q_raw[j][:].rearrange("p j w -> p w j"))
            codes = pool.tile([P, Q], U32, name="q_words%d" % j, align_bytes=64)
            scales = pool.tile([P, Q], U8, name="q_scales%d" % j, align_bytes=64)
            nc.vector.quantize_mx(
                out=codes[:].bitcast(FP8X4), scales=scales[:], in_=grouped[:].rearrange("p w j -> p (w j)")
            )
            q_words.append(codes)
            q_scales.append(scales)

        scores = [pool.tile([P, T], F32, name="scores%d" % j, tag="scores%d" % j) for j in range(2)]
        for j in range(2):
            for n in range(T // N_MM):
                bank = psum.tile([P, N_MM], F32, name="bank%d_%d" % (j, n))
                load, col = divmod(n * N_MM, key_cols)
                cols = slice(n * N_MM, (n + 1) * N_MM)
                nc.tensor.matmul_mx(
                    out=bank[:],
                    lhsT=q_words[j][:].bitcast(FP8X4),
                    lhsT_scale=q_scales[j][:],
                    rhs=k_words[load][:, col : col + N_MM].bitcast(FP8X4),
                    rhs_scale=k_scales[:, cols],
                    start=True,
                    stop=True,
                )
                if j == 1 or n % 2 == 0:
                    nc.scalar.activation(scores[j][:, cols], bank[:], ACT.Copy)
                else:
                    nc.vector.tensor_copy(scores[j][:, cols], bank[:])

        half, half_cols = SLOTS // 2, LIST_COLS // 2
        halves = [slice(h * half, (h + 1) * half) for h in range(2)]
        lists = [list_ab[:, h * half_cols : (h + 1) * half_cols] for h in range(2)]
        a_at = pool.tile([P, SLOTS], F32, name="a_at")
        b_at = pool.tile([P, SLOTS], F32, name="b_at")
        exp_a = pool.tile([P, SLOTS], F32, name="exp_a", tag="keys1", align_bytes=64)
        exp_b = pool.tile([P, SLOTS], F32, name="exp_b", tag="exp_b")
        for h in range(2):
            nc.vector.tensor_copy(a_at[:, halves[h]], scores[0][:].indirect(lists[h]))
        for h in range(2):
            nc.vector.tensor_copy(b_at[:, halves[h]], scores[1][:].indirect(lists[h]))
        nc.scalar.activation(exp_a[:, halves[0]], a_at[:, halves[0]], ACT.Exp)
        nc.scalar.activation(exp_b[:, halves[1]], scores[1][:].indirect(lists[1]), ACT.Exp)
        nc.scalar.activation(exp_a[:, halves[1]], a_at[:, halves[1]], ACT.Exp)
        nc.scalar.activation(exp_b[:, halves[0]], b_at[:, halves[0]], ACT.Exp)
        old_at = pool.tile([P, SLOTS], F32, name="old_at", tag="scores1")
        nc.vector.tensor_copy(old_at[:], old_sb[:].indirect(list_old[:]))

        diff = pool.tile([P, SLOTS], F32, name="diff")
        gap = pool.tile([P, SLOTS], F32, name="gap")
        log_b = pool.tile([P, SLOTS], F32, name="log_b")
        soft_a = pool.tile([P, SLOTS], F32, name="soft_a")
        soft_b = pool.tile([P, SLOTS], F32, name="soft_b")
        both = pool.tile([P, SLOTS], F32, name="both")
        nc.vector.tensor_tensor(diff[:], a_at[:], b_at[:], ALU.subtract)
        nc.vector.scalar_tensor_tensor(gap[:], diff[:], -1.0, diff[:], ALU.mult, ALU.max)
        nc.scalar.activation(log_b[:], exp_b[:], ACT.Ln, bias=1.0)
        log_a = pool.tile([P, SLOTS], F32, name="log_a", tag="exp_b")
        nc.scalar.activation(log_a[:], exp_a[:], ACT.Ln, bias=1.0)
        nc.vector.scalar_tensor_tensor(soft_b[:], log_b[:], SOFTPLUS_CAP, b_at[:], ALU.min, ALU.max)
        for s in halves:
            nc.vector.scalar_tensor_tensor(soft_a[:, s], log_a[:, s], SOFTPLUS_CAP, a_at[:, s], ALU.min, ALU.max)
        for s in halves:
            nc.vector.tensor_tensor(both[:, s], soft_a[:, s], soft_b[:, s], ALU.mult)

        root = pool.tile([P, SLOTS], F32, name="root")
        weight = pool.tile([P, SLOTS], F32, name="weight")
        for s in halves:
            nc.scalar.activation(root[:, s], both[:, s], ACT.Sqrt, bias=0.1)
            nc.vector.scalar_tensor_tensor(weight[:, s], root[:, s], lam_sb[:], gap[:, s], ALU.mult, ALU.subtract)
        nc.vector.tensor_tensor(placed[:].indirect(list_out[:]), weight[:], old_at[:], ALU.mult)

        result = pool.tile([P, T], F32, name="result")
        width = T // STORES
        for n in range(STORES):
            cols = slice(n * width, (n + 1) * width)
            nc.vector.tensor_tensor(result[:, cols], placed[:, cols], base_sb[:, cols], ALU.add)
            queue = nc.sync if n % 2 == 0 else nc.scalar
            queue.dma_start(out[:, cols], result[:, cols])
